import numpy as np
import ml_dtypes


def mxq(x, axis, fmt="e4m3"):
    dtype, down = {"e4m3": (ml_dtypes.float8_e4m3fn, 7), "e5m2": (ml_dtypes.float8_e5m2, 14)}[fmt]
    v = np.moveaxis(np.asarray(x, np.float32).astype(ml_dtypes.bfloat16).astype(np.float64), axis, -1)
    blocks = v.reshape(v.shape[:-1] + (-1, 32))
    amax = np.abs(blocks).max(-1, keepdims=True)
    byte = np.maximum(np.where(amax > 0, np.frexp(amax)[1] - 1 + 127, 0) - down, 1)
    scale = np.exp2(byte - 127.0)
    codes = (blocks / scale).astype(np.float32).astype(dtype).astype(np.float64)
    return np.moveaxis((codes * scale).reshape(v.shape), -1, axis)


WIDE = False


def mx_kscale(k):
    if not WIDE:
        return np.ones(k)
    levels = np.array([10, -10, 5, -5, 0])
    if k % 512:
        return np.exp2(np.random.permutation(np.resize(levels, k // 32))).repeat(32)
    a = np.empty((k // 512, 16))
    for p in range(k // 512):
        a[p, :8] = np.random.permutation(np.resize(levels, 8))
        for g in range(8):
            far = levels[np.abs(levels - a[p, g]) >= 10]
            a[p, g + 8] = far[np.random.randint(len(far))]
    return np.exp2(a.ravel()).repeat(32)


def f64(x):
    return np.asarray(x).astype(np.float64)


def striped8(idx):
    return np.asarray(idx).reshape(8, -1, 16).transpose(0, 2, 1).reshape(128, -1).astype(np.uint16)


def unstriped8(offs):
    return offs.reshape(8, 16, -1).transpose(0, 2, 1).reshape(8, -1).astype(np.int64)


def pick8(x, idx, run):
    r = np.arange(len(x))
    return x[r[:, None], idx[r % (8 * run) // run]]


E2M1 = np.array([0.0, 0.5, 1.0, 1.5, 2.0, 3.0, 4.0, 6.0, -0.0, -0.5, -1.0, -1.5, -2.0, -3.0, -4.0, -6.0])


def pack_weight(w, fmt):
    k, n = w.shape
    w = f64(np.asarray(w, np.float32).astype(ml_dtypes.bfloat16)).reshape(k // 32, 32, n)
    amax = np.abs(w).max(1)
    if fmt == "e4m3":
        byte = np.frexp(amax)[1] - 1 + 127 - 7
    else:
        mant, ex = np.frexp(amax / 6.0)
        byte = np.where(mant > 0.5, ex, ex - 1) + 127
    byte = np.clip(np.where(amax > 0, byte, 1), 1, 254)
    scaled = (w * np.exp2(127.0 - byte)[:, None, :]).reshape(k, n).astype(np.float32)
    by_word = np.ascontiguousarray(scaled.reshape(k // 512, 128, 4, n).transpose(0, 1, 3, 2))
    if fmt == "e4m3":
        words = by_word.astype(ml_dtypes.float8_e4m3fn).view(np.uint8)
    else:
        c = by_word.astype(ml_dtypes.float4_e2m1fn).view(np.uint8) & 0xF
        words = (c[..., 0::2] | (c[..., 1::2] << 4)).reshape(k // 512, 128, 2 * n)
    return np.ascontiguousarray(words), np.ascontiguousarray(byte.astype(np.uint8).reshape(k // 512, 16, n))


def unpack_weight(words, scales, fmt):
    g, _, n = scales.shape
    words = np.ascontiguousarray(words).reshape(g, 128, n, -1)
    if fmt == "e4m3":
        vals = words.view(ml_dtypes.float8_e4m3fn).astype(np.float64)
    else:
        nib = np.empty((g, 128, n, 4), np.uint8)
        nib[..., 0::2] = words & 0xF
        nib[..., 1::2] = words >> 4
        vals = E2M1[nib]
    vals = vals * np.repeat(np.exp2(scales.astype(np.float64) - 127.0), 8, axis=1)[..., None]
    return vals.transpose(0, 1, 3, 2).reshape(g * 512, n)


D, K, T, I, Q = 512, 512, 1024, 512, 128


def setup_inputs():
    n = np.random.standard_normal
    idx = np.stack([np.random.permutation(T)[:I] for _ in range(8)])
    idx2 = np.stack([np.random.permutation(T)[:I] for _ in range(8)])
    idx3 = np.stack([np.random.permutation(T)[:I] for _ in range(8)])
    idx4 = np.stack([np.random.permutation(T)[:I] for _ in range(8)])
    idx5 = np.stack([np.random.permutation(T)[:I] for _ in range(8)])
    fd = mx_kscale(D)
    fk = mx_kscale(K)
    wqp = pack_weight(n((D, K)) * 1.0 / np.sqrt(D) * fd[:, None] * fk, "e4m3")
    cachep = pack_weight(n((K, T)) * 1.0 / np.sqrt(K) / fk[:, None], "e4m3")
    tagsp = pack_weight(n((D, T)) * 0.5 / np.sqrt(D) * fd[:, None], "e2m1")
    return {
        "states": (n((D, Q)) * 0.95 / fd[:, None]).astype(np.float32),
        "wq_words": wqp[0],
        "wq_scales": wqp[1],
        "cache_words": cachep[0],
        "cache_scales": cachep[1],
        "tags_words": tagsp[0],
        "tags_scales": tagsp[1],
        "offs": striped8(idx),
        "offs2": striped8(idx2),
        "offs3": striped8(idx3),
        "offs4": striped8(idx4),
        "offs5": striped8(idx5),
    }


def reference(states, wq_words, wq_scales, cache_words, cache_scales, tags_words, tags_scales, offs, offs2, offs3, offs4, offs5):
    idx = unstriped8(offs)
    idx2 = unstriped8(offs2)
    idx3 = unstriped8(offs3)
    idx4 = unstriped8(offs4)
    idx5 = unstriped8(offs5)
    wqu = unpack_weight(wq_words, wq_scales, "e4m3")
    cacheu = unpack_weight(cache_words, cache_scales, "e4m3")
    tagsu = unpack_weight(tags_words, tags_scales, "e2m1")
    statesq = mxq(f64(states), 0, "e4m3")
    qv = wqu.T @ statesq
    qvq = mxq(qv, 0, "e4m3")
    a = qvq.T @ cacheu + statesq.T @ tagsu
    f1 = np.zeros((Q, T))
    f1[np.arange(Q)[:, None], idx2[np.arange(Q) % 128 // 16]] = pick8(a, idx, 16)
    c1 = a - f1
    f2 = np.zeros((Q, T))
    f2[np.arange(Q)[:, None], idx[np.arange(Q) % 128 // 16]] = pick8(c1, idx3, 16)
    c2 = np.maximum(c1, f2)
    y = pick8(c2, idx4, 16) + pick8(c1, idx5, 16)
    return y

@@ -1,0 +1,140 @@
+from contextlib import ExitStack
+
+import concourse.mybir as mybir
+
+D, K, T, SLOTS, Q = 512, 512, 1024, 512, 128
+FLOPS = 2 * D * K * Q + 2 * K * Q * T + 2 * D * Q * T
+
+F32 = mybir.dt.float32
+BF16 = mybir.dt.bfloat16
+I32 = mybir.dt.int32
+U32 = mybir.dt.uint32
+U16 = mybir.dt.uint16
+U8 = mybir.dt.uint8
+FP8X4 = mybir.dt.float8_e4m3fn_x4
+FP4X4 = mybir.dt.float4_e2m1fn_x4
+COPY = mybir.ActivationFunctionType.Copy
+ALU = mybir.AluOpType
+
+P = 128
+PACK = 4
+CHUNK = 256
+HALF = SLOTS // 2
+HCOL = HALF // 16
+
+
+def tile_attend_backpair_parts_kernel(tc, states, wq_words, wq_scales, cache_words, cache_scales, tags_words,
+                                       tags_scales, offs, offs2, offs3, offs4, offs5, out):
+    nc = tc.nc
+    with ExitStack() as ctx:
+        sb = ctx.enter_context(tc.tile_pool(name="sb", bufs=1))
+        ps = ctx.enter_context(tc.psum_pool(name="ps", bufs=1))
+
+        def plane_tile(name, n):
+            t = sb.tile([P, 2 * n], U8, name=name, align_bytes=64)
+            nc.vector.memset(t[:].bitcast(I32), 0)
+            return t
+
+        def load_plane(t, scales, n):
+            rows = scales[0].bitcast(I32).rearrange("(h q r) n -> q r h n", h=2, q=2)
+            for q in range(2):
+                nc.sync.dma_start(out=t[32 * q:32 * q + 4, :].bitcast(I32).rearrange("r (h n) -> r h n", h=2), in_=rows[q])
+
+        def finish_plane(t, n):
+            w = t[:].bitcast(I32)
+            nc.vector.tensor_copy(out=w[64:128, 0:n // 4], in_=w[0:64, n // 4:n // 2])
+
+        wq_s = plane_tile("wq_s", K)
+        tags_s = plane_tile("tags_s", T)
+        cache_s = plane_tile("cache_s", T)
+        st_raw = sb.tile([P, PACK, Q], F32, name="st_raw")
+        nc.sync.dma_start(out=st_raw[:], in_=states.rearrange("(p j) q -> p j q", j=PACK))
+        load_plane(wq_s, wq_scales, K)
+        wq_raw = sb.tile([P, K], U32, name="wq_raw", align_bytes=64)
+        nc.sync.dma_start(out=wq_raw[:].bitcast(I32), in_=wq_words[0].rearrange("p n t -> p (n t)").bitcast(I32))
+        load_plane(tags_s, tags_scales, T)
+        tags_w = sb.tile([P, 2 * T], U8, name="tags_w", align_bytes=64)
+        nc.sync.dma_start(out=tags_w[:].bitcast(I32), in_=tags_words[0].bitcast(I32))
+        cache_w = sb.tile([P, T], U32, name="cache_w", align_bytes=64)
+        nc.sync.dma_start(out=cache_w[:].bitcast(I32), in_=cache_words[0].rearrange("p n t -> p (n t)").bitcast(I32))
+        load_plane(cache_s, cache_scales, T)
+        lists = []
+        for n, src in enumerate((offs, offs2, offs3, offs4, offs5)):
+            lt = sb.tile([P, SLOTS // 16], U16, name="list%d" % n)
+            nc.sync.dma_start(lt[:], src)
+            lists.append(lt)
+        l1, l2, l3, l4, l5 = lists
+
+        f1 = sb.tile([P, T], F32, name="f1")
+        f2 = sb.tile([P, T], F32, name="f2")
+        nc.vector.memset(f1[:], 0.0)
+        nc.vector.memset(f2[:], 0.0)
+
+        finish_plane(wq_s, K)
+        st_bf = sb.tile([P, Q, PACK], BF16, name="st_bf", align_bytes=64)
+        hq = Q // 2
+        nc.vector.tensor_copy(out=st_bf[:, 0:hq, :], in_=st_raw[:, :, 0:hq].rearrange("p j q -> p q j"))
+        nc.scalar.activation(st_bf[:, hq:Q, :], st_raw[:, :, hq:Q].rearrange("p j q -> p q j"), COPY)
+        wq_sd = sb.tile([P, K], U8, name="wq_sd", align_bytes=64)
+        nc.vector.tensor_copy(out=wq_sd[:].rearrange("p (t b i) -> p b t i", t=PACK, i=16),
+                              in_=wq_s[:, 0:K].rearrange("p (b i t) -> p b t i", t=PACK, i=16))
+        st_c = sb.tile([P, Q], U32, name="st_c", align_bytes=64)
+        st_s = sb.tile([P, Q], U8, name="st_s", align_bytes=64)
+        nc.vector.quantize_mx(out=st_c[:].bitcast(FP8X4), scales=st_s[:], in_=st_bf[:].rearrange("p q j -> p (q j)"))
+        wq_d = sb.tile([P, PACK, P], U32, name="wq_d", align_bytes=64)
+        src = wq_raw[:].rearrange("p (b i t) -> p b t i", t=PACK, i=4)
+        dst = wq_d[:].rearrange("p t (b i) -> p b t i", i=4)
+        nc.scalar.copy(dst[:, 0:16], src[:, 0:16])
+        nc.vector.tensor_copy(out=dst[:, 16:32], in_=src[:, 16:32])
+
+        qv_ps = ps.tile([P, PACK, Q], F32, name="qv_ps")
+        for t in range(PACK):
+            nc.tensor.matmul_mx(out=qv_ps[:, t, :], lhsT=wq_d[:, t, :].bitcast(FP8X4), lhsT_scale=wq_sd[:, t * P:(t + 1) * P],
+                                rhs=st_c[:].bitcast(FP8X4), rhs_scale=st_s[:], start=True, stop=True)
+        finish_plane(tags_s, T)
+        finish_plane(cache_s, T)
+        nch = T // CHUNK
+        a_ps = [ps.tile([P, CHUNK], F32, name="a_ps%d" % c) for c in range(nch)]
+        for c in range(nch):
+            nc.tensor.matmul_mx(out=a_ps[c][:], lhsT=st_c[:].bitcast(FP8X4), lhsT_scale=st_s[:],
+                                rhs=tags_w[:, 2 * c * CHUNK:2 * (c + 1) * CHUNK].bitcast(FP4X4),
+                                rhs_scale=tags_s[:, c * CHUNK:(c + 1) * CHUNK], start=True, stop=False)
+        qv_bf = sb.tile([P, Q, PACK], BF16, name="qv_bf", align_bytes=64)
+        nc.scalar.activation(qv_bf[:], qv_ps[:].rearrange("p t q -> p q t"), COPY)
+        qv_c = sb.tile([P, Q], U32, name="qv_c", align_bytes=64)
+        qv_s = sb.tile([P, Q], U8, name="qv_s", align_bytes=64)
+        nc.vector.quantize_mx(out=qv_c[:].bitcast(FP8X4), scales=qv_s[:], in_=qv_bf[:].rearrange("p q j -> p (q j)"))
+        a = sb.tile([P, T], F32, name="a")
+        for c in range(nch):
+            cols = slice(c * CHUNK, (c + 1) * CHUNK)
+            nc.tensor.matmul_mx(out=a_ps[c][:], lhsT=qv_c[:].bitcast(FP8X4), lhsT_scale=qv_s[:],
+                                rhs=cache_w[:, cols].bitcast(FP8X4), rhs_scale=cache_s[:, cols], start=False, stop=True)
+            if c % 2 == 0:
+                nc.vector.tensor_copy(out=a[:, cols], in_=a_ps[c][:])
+            else:
+                nc.scalar.activation(a[:, cols], a_ps[c][:], COPY)
+
+        def gather_halves(name, window, lst):
+            g = sb.tile([P, SLOTS], F32, name=name)
+            nc.vector.tensor_copy(out=g[:, 0:HALF], in_=window[:].indirect(lst[:, 0:HCOL]))
+            nc.scalar.activation(g[:, HALF:SLOTS], window[:].indirect(lst[:, HCOL:2 * HCOL]), COPY)
+            return g
+
+        g1 = gather_halves("g1", a, l1)
+        nc.scalar.activation(f1[:].indirect(l2[:]), g1[:], COPY)
+        c1 = sb.tile([P, T], F32, name="c1")
+        nc.vector.tensor_tensor(c1[:], a[:], f1[:], ALU.subtract)
+        g3 = gather_halves("g3", c1, l3)
+        nc.scalar.activation(f2[:].indirect(l1[:]), g3[:], COPY)
+        g5 = sb.tile([P, SLOTS], F32, name="g5")
+        nc.vector.tensor_copy(out=g5[:], in_=c1[:].indirect(l5[:]))
+        c2 = sb.tile([P, T], F32, name="c2")
+        nc.vector.tensor_tensor(c2[:], c1[:], f2[:], ALU.max)
+        y0 = sb.tile([P, HALF], F32, name="y0")
+        y1 = sb.tile([P, HALF], F32, name="y1")
+        g4 = sb.tile([P, HALF], F32, name="g4")
+        nc.vector.tensor_tensor(y0[:], c2[:].indirect(l4[:, 0:HCOL]), g5[:, 0:HALF], ALU.add)
+        nc.scalar.activation(g4[:], c2[:].indirect(l4[:, HCOL:2 * HCOL]), COPY)
+        nc.sync.dma_start(out=out[:, 0:HALF], in_=y0[:])
+        nc.vector.tensor_tensor(y1[:], g4[:], g5[:, HALF:SLOTS], ALU.add)
+        nc.sync.dma_start(out=out[:, HALF:SLOTS], in_=y1[:])

@@ -66,13 +66,11 @@ def tile_attend_backpair_parts_kernel(tc, states, wq_words, wq_scales, cache_wor
         l1, l2, l3, l4, l5 = lists
 
         f1 = sb.tile([P, T], F32, name="f1")
-        f2 = sb.tile([P, T], F32, name="f2")
         nc.vector.memset(f1[:], 0.0)
-        nc.vector.memset(f2[:], 0.0)
 
         finish_plane(wq_s, K)
         st_bf = sb.tile([P, Q, PACK], BF16, name="st_bf", align_bytes=64)
-        hq = Q // 2
+        hq = 96
         nc.vector.tensor_copy(out=st_bf[:, 0:hq, :], in_=st_raw[:, :, 0:hq].rearrange("p j q -> p q j"))
         nc.scalar.activation(st_bf[:, hq:Q, :], st_raw[:, :, hq:Q].rearrange("p j q -> p q j"), COPY)
         wq_sd = sb.tile([P, K], U8, name="wq_sd", align_bytes=64)
@@ -104,7 +102,7 @@ def tile_attend_backpair_parts_kernel(tc, states, wq_words, wq_scales, cache_wor
         qv_c = sb.tile([P, Q], U32, name="qv_c", align_bytes=64)
         qv_s = sb.tile([P, Q], U8, name="qv_s", align_bytes=64)
         nc.vector.quantize_mx(out=qv_c[:].bitcast(FP8X4), scales=qv_s[:], in_=qv_bf[:].rearrange("p q j -> p (q j)"))
-        a = sb.tile([P, T], F32, name="a")
+        a = sb.tile([P, T], F32, name="a", tag="a_f2")
         for c in range(nch):
             cols = slice(c * CHUNK, (c + 1) * CHUNK)
             nc.tensor.matmul_mx(out=a_ps[c][:], lhsT=qv_c[:].bitcast(FP8X4), lhsT_scale=qv_s[:],
@@ -122,8 +120,12 @@ def tile_attend_backpair_parts_kernel(tc, states, wq_words, wq_scales, cache_wor
 
         g1 = gather_halves("g1", a, l1)
         nc.scalar.activation(f1[:].indirect(l2[:]), g1[:], COPY)
+        f2 = sb.tile([P, T], F32, name="f2", tag="a_f2")
+        nc.vector.memset(f2[:], 0.0)
         c1 = sb.tile([P, T], F32, name="c1")
-        nc.vector.tensor_tensor(c1[:], a[:], f1[:], ALU.subtract)
+        for c in range(nch):
+            cols = slice(c * CHUNK, (c + 1) * CHUNK)
+            nc.vector.tensor_tensor(c1[:, cols], a_ps[c][:], f1[:, cols], ALU.subtract)
         g3 = gather_halves("g3", c1, l3)
         nc.scalar.activation(f2[:].indirect(l1[:]), g3[:], COPY)
         g5 = sb.tile([P, SLOTS], F32, name="g5")

@@ -46,7 +46,8 @@ def tile_attend_backpair_parts_kernel(tc, states, wq_words, wq_scales, cache_wor
 
         wq_s = plane_tile("wq_s", K)
         tags_s = plane_tile("tags_s", T)
-        cache_s = plane_tile("cache_s", T)
+        cache_s = sb.tile([P, CHUNK], U8, name="cache_s", align_bytes=64)
+        nc.vector.memset(cache_s[:].bitcast(I32), 0)
         st_raw = sb.tile([P, PACK, Q], F32, name="st_raw")
         nc.sync.dma_start(out=st_raw[:], in_=states.rearrange("(p j) q -> p j q", j=PACK))
         load_plane(wq_s, wq_scales, K)
@@ -57,7 +58,9 @@ def tile_attend_backpair_parts_kernel(tc, states, wq_words, wq_scales, cache_wor
         nc.sync.dma_start(out=tags_w[:].bitcast(I32), in_=tags_words[0].bitcast(I32))
         cache_w = sb.tile([P, T], U32, name="cache_w", align_bytes=64)
         nc.sync.dma_start(out=cache_w[:].bitcast(I32), in_=cache_words[0].rearrange("p n t -> p (n t)").bitcast(I32))
-        load_plane(cache_s, cache_scales, T)
+        for quad in range(4):
+            nc.sync.dma_start(out=cache_s[32 * quad:32 * quad + 16, :].bitcast(I32),
+                              in_=cache_scales[0].bitcast(I32)[4 * quad:4 * quad + 4, :].rearrange("r (c n) -> c r n", c=4))
         lists = []
         for n, src in enumerate((offs, offs2, offs3, offs4, offs5)):
             lt = sb.tile([P, SLOTS // 16], U16, name="list%d" % n)
@@ -90,7 +93,6 @@ def tile_attend_backpair_parts_kernel(tc, states, wq_words, wq_scales, cache_wor
             nc.tensor.matmul_mx(out=qv_ps[:, t, :], lhsT=wq_d[:, t, :].bitcast(FP8X4), lhsT_scale=wq_sd[:, t * P:(t + 1) * P],
                                 rhs=st_c[:].bitcast(FP8X4), rhs_scale=st_s[:], start=True, stop=True)
         finish_plane(tags_s, T)
-        finish_plane(cache_s, T)
         nch = T // CHUNK
         a_ps = [ps.tile([P, CHUNK], F32, name="a_ps%d" % c) for c in range(nch)]
         for c in range(nch):
@@ -106,7 +108,7 @@ def tile_attend_backpair_parts_kernel(tc, states, wq_words, wq_scales, cache_wor
         for c in range(nch):
             cols = slice(c * CHUNK, (c + 1) * CHUNK)
             nc.tensor.matmul_mx(out=a_ps[c][:], lhsT=qv_c[:].bitcast(FP8X4), lhsT_scale=qv_s[:],
-                                rhs=cache_w[:, cols].bitcast(FP8X4), rhs_scale=cache_s[:, cols], start=False, stop=True)
+                                rhs=cache_w[:, cols].bitcast(FP8X4), rhs_scale=cache_s[4 * c:P, :], start=False, stop=True)
             if c % 2 == 0:
                 nc.vector.tensor_copy(out=a[:, cols], in_=a_ps[c][:])
             else:

from contextlib import ExitStack

import concourse.mybir as mybir

D, K, T, SLOTS, Q = 512, 512, 1024, 512, 128
FLOPS = 2 * D * K * Q + 2 * K * Q * T + 2 * D * Q * T

F32 = mybir.dt.float32
BF16 = mybir.dt.bfloat16
I32 = mybir.dt.int32
U32 = mybir.dt.uint32
U16 = mybir.dt.uint16
U8 = mybir.dt.uint8
FP8X4 = mybir.dt.float8_e4m3fn_x4
FP4X4 = mybir.dt.float4_e2m1fn_x4
COPY = mybir.ActivationFunctionType.Copy
ALU = mybir.AluOpType

P = 128
PACK = 4
CHUNK = 256
HALF = SLOTS // 2
HCOL = HALF // 16


def tile_attend_backpair_parts_kernel(tc, states, wq_words, wq_scales, cache_words, cache_scales, tags_words,
                                       tags_scales, offs, offs2, offs3, offs4, offs5, out):
    nc = tc.nc
    with ExitStack() as ctx:
        sb = ctx.enter_context(tc.tile_pool(name="sb", bufs=1))
        ps = ctx.enter_context(tc.psum_pool(name="ps", bufs=1))

        def plane_tile(name, n):
            t = sb.tile([P, 2 * n], U8, name=name, align_bytes=64)
            nc.vector.memset(t[:].bitcast(I32), 0)
            return t

        def load_plane(t, scales, n):
            rows = scales[0].bitcast(I32).rearrange("(h q r) n -> q r h n", h=2, q=2)
            for q in range(2):
                nc.sync.dma_start(out=t[32 * q:32 * q + 4, :].bitcast(I32).rearrange("r (h n) -> r h n", h=2), in_=rows[q])

        def finish_plane(t, n):
            w = t[:].bitcast(I32)
            nc.vector.tensor_copy(out=w[64:128, 0:n // 4], in_=w[0:64, n // 4:n // 2])

        wq_s = plane_tile("wq_s", K)
        tags_s = plane_tile("tags_s", T)
        cache_s = sb.tile([P, CHUNK], U8, name="cache_s", align_bytes=64)
        nc.vector.memset(cache_s[:].bitcast(I32), 0)
        st_raw = sb.tile([P, PACK, Q], F32, name="st_raw")
        nc.sync.dma_start(out=st_raw[:], in_=states.rearrange("(p j) q -> p j q", j=PACK))
        load_plane(wq_s, wq_scales, K)
        wq_raw = sb.tile([P, K], U32, name="wq_raw", align_bytes=64)
        nc.sync.dma_start(out=wq_raw[:].bitcast(I32), in_=wq_words[0].rearrange("p n t -> p (n t)").bitcast(I32))
        load_plane(tags_s, tags_scales, T)
        tags_w = sb.tile([P, 2 * T], U8, name="tags_w", align_bytes=64)
        nc.sync.dma_start(out=tags_w[:].bitcast(I32), in_=tags_words[0].bitcast(I32))
        cache_w = sb.tile([P, T], U32, name="cache_w", align_bytes=64)
        nc.sync.dma_start(out=cache_w[:].bitcast(I32), in_=cache_words[0].rearrange("p n t -> p (n t)").bitcast(I32))
        for quad in range(4):
            nc.sync.dma_start(out=cache_s[32 * quad:32 * quad + 16, :].bitcast(I32),
                              in_=cache_scales[0].bitcast(I32)[4 * quad:4 * quad + 4, :].rearrange("r (c n) -> c r n", c=4))
        lists = []
        for n, src in enumerate((offs, offs2, offs3, offs4, offs5)):
            lt = sb.tile([P, SLOTS // 16], U16, name="list%d" % n)
            nc.sync.dma_start(lt[:], src)
            lists.append(lt)
        l1, l2, l3, l4, l5 = lists

        f1 = sb.tile([P, T], F32, name="f1")
        nc.vector.memset(f1[:], 0.0)

        finish_plane(wq_s, K)
        st_bf = sb.tile([P, Q, PACK], BF16, name="st_bf", align_bytes=64)
        hq = 96
        nc.vector.tensor_copy(out=st_bf[:, 0:hq, :], in_=st_raw[:, :, 0:hq].rearrange("p j q -> p q j"))
        nc.scalar.activation(st_bf[:, hq:Q, :], st_raw[:, :, hq:Q].rearrange("p j q -> p q j"), COPY)
        wq_sd = sb.tile([P, K], U8, name="wq_sd", align_bytes=64)
        nc.vector.tensor_copy(out=wq_sd[:].rearrange("p (t b i) -> p b t i", t=PACK, i=16),
                              in_=wq_s[:, 0:K].rearrange("p (b i t) -> p b t i", t=PACK, i=16))
        st_c = sb.tile([P, Q], U32, name="st_c", align_bytes=64)
        st_s = sb.tile([P, Q], U8, name="st_s", align_bytes=64)
        nc.vector.quantize_mx(out=st_c[:].bitcast(FP8X4), scales=st_s[:], in_=st_bf[:].rearrange("p q j -> p (q j)"))
        wq_d = sb.tile([P, PACK, P], U32, name="wq_d", align_bytes=64)
        src = wq_raw[:].rearrange("p (b i t) -> p b t i", t=PACK, i=4)
        dst = wq_d[:].rearrange("p t (b i) -> p b t i", i=4)
        nc.scalar.copy(dst[:, 0:16], src[:, 0:16])
        nc.vector.tensor_copy(out=dst[:, 16:32], in_=src[:, 16:32])

        qv_ps = ps.tile([P, PACK, Q], F32, name="qv_ps")
        for t in range(PACK):
            nc.tensor.matmul_mx(out=qv_ps[:, t, :], lhsT=wq_d[:, t, :].bitcast(FP8X4), lhsT_scale=wq_sd[:, t * P:(t + 1) * P],
                                rhs=st_c[:].bitcast(FP8X4), rhs_scale=st_s[:], start=True, stop=True)
        finish_plane(tags_s, T)
        nch = T // CHUNK
        a_ps = [ps.tile([P, CHUNK], F32, name="a_ps%d" % c) for c in range(nch)]
        for c in range(nch):
            nc.tensor.matmul_mx(out=a_ps[c][:], lhsT=st_c[:].bitcast(FP8X4), lhsT_scale=st_s[:],
                                rhs=tags_w[:, 2 * c * CHUNK:2 * (c + 1) * CHUNK].bitcast(FP4X4),
                                rhs_scale=tags_s[:, c * CHUNK:(c + 1) * CHUNK], start=True, stop=False)
        qv_bf = sb.tile([P, Q, PACK], BF16, name="qv_bf", align_bytes=64)
        nc.scalar.activation(qv_bf[:], qv_ps[:].rearrange("p t q -> p q t"), COPY)
        qv_c = sb.tile([P, Q], U32, name="qv_c", align_bytes=64)
        qv_s = sb.tile([P, Q], U8, name="qv_s", align_bytes=64)
        nc.vector.quantize_mx(out=qv_c[:].bitcast(FP8X4), scales=qv_s[:], in_=qv_bf[:].rearrange("p q j -> p (q j)"))
        a = sb.tile([P, T], F32, name="a", tag="a_f2")
        for c in range(nch):
            cols = slice(c * CHUNK, (c + 1) * CHUNK)
            nc.tensor.matmul_mx(out=a_ps[c][:], lhsT=qv_c[:].bitcast(FP8X4), lhsT_scale=qv_s[:],
                                rhs=cache_w[:, cols].bitcast(FP8X4), rhs_scale=cache_s[4 * c:P, :], start=False, stop=True)
            if c % 2 == 0:
                nc.vector.tensor_copy(out=a[:, cols], in_=a_ps[c][:])
            else:
                nc.scalar.activation(a[:, cols], a_ps[c][:], COPY)

        def gather_halves(name, window, lst):
            g = sb.tile([P, SLOTS], F32, name=name)
            nc.vector.tensor_copy(out=g[:, 0:HALF], in_=window[:].indirect(lst[:, 0:HCOL]))
            nc.scalar.activation(g[:, HALF:SLOTS], window[:].indirect(lst[:, HCOL:2 * HCOL]), COPY)
            return g

        g1 = gather_halves("g1", a, l1)
        nc.scalar.activation(f1[:].indirect(l2[:]), g1[:], COPY)
        f2 = sb.tile([P, T], F32, name="f2", tag="a_f2")
        nc.vector.memset(f2[:], 0.0)
        c1 = sb.tile([P, T], F32, name="c1")
        for c in range(nch):
            cols = slice(c * CHUNK, (c + 1) * CHUNK)
            nc.vector.tensor_tensor(c1[:, cols], a_ps[c][:], f1[:, cols], ALU.subtract)
        g3 = gather_halves("g3", c1, l3)
        nc.scalar.activation(f2[:].indirect(l1[:]), g3[:], COPY)
        g5 = sb.tile([P, SLOTS], F32, name="g5")
        nc.vector.tensor_copy(out=g5[:], in_=c1[:].indirect(l5[:]))
        c2 = sb.tile([P, T], F32, name="c2")
        nc.vector.tensor_tensor(c2[:], c1[:], f2[:], ALU.max)
        y0 = sb.tile([P, HALF], F32, name="y0")
        y1 = sb.tile([P, HALF], F32, name="y1")
        g4 = sb.tile([P, HALF], F32, name="g4")
        nc.vector.tensor_tensor(y0[:], c2[:].indirect(l4[:, 0:HCOL]), g5[:, 0:HALF], ALU.add)
        nc.scalar.activation(g4[:], c2[:].indirect(l4[:, HCOL:2 * HCOL]), COPY)
        nc.sync.dma_start(out=out[:, 0:HALF], in_=y0[:])
        nc.vector.tensor_tensor(y1[:], g4[:], g5[:, HALF:SLOTS], ALU.add)
        nc.sync.dma_start(out=out[:, HALF:SLOTS], in_=y1[:])
